import numpy as np
import ml_dtypes


def mxq(x, axis, fmt="e4m3"):
    dtype, down = {"e4m3": (ml_dtypes.float8_e4m3fn, 7), "e5m2": (ml_dtypes.float8_e5m2, 14)}[fmt]
    v = np.moveaxis(np.asarray(x, np.float32).astype(ml_dtypes.bfloat16).astype(np.float64), axis, -1)
    blocks = v.reshape(v.shape[:-1] + (-1, 32))
    amax = np.abs(blocks).max(-1, keepdims=True)
    byte = np.maximum(np.where(amax > 0, np.frexp(amax)[1] - 1 + 127, 0) - down, 1)
    scale = np.exp2(byte - 127.0)
    codes = (blocks / scale).astype(np.float32).astype(dtype).astype(np.float64)
    return np.moveaxis((codes * scale).reshape(v.shape), -1, axis)


WIDE = False


def mx_kscale(k):
    if not WIDE:
        return np.ones(k)
    levels = np.array([10, -10, 5, -5, 0])
    if k % 512:
        return np.exp2(np.random.permutation(np.resize(levels, k // 32))).repeat(32)
    a = np.empty((k // 512, 16))
    for p in range(k // 512):
        a[p, :8] = np.random.permutation(np.resize(levels, 8))
        for g in range(8):
            far = levels[np.abs(levels - a[p, g]) >= 10]
            a[p, g + 8] = far[np.random.randint(len(far))]
    return np.exp2(a.ravel()).repeat(32)


def f64(x):
    return np.asarray(x).astype(np.float64)


def striped(idx):
    return np.tile(idx.reshape(-1, 16).T, (8, 1)).astype(np.uint16)


def unstriped(offs):
    return offs[:16].T.reshape(-1).astype(np.int64)


def striped8(idx):
    return np.concatenate([x.reshape(-1, 16).T for x in idx]).astype(np.uint16)


def runs(offs, k):
    lists = np.stack([offs[16 * r : 16 * r + 16].T.reshape(-1) for r in range(8)]).astype(np.int64)
    return lists[np.arange(k) % 512 // 64]


def pack_weight(w):
    k, n = w.shape
    w = f64(np.asarray(w, np.float32).astype(ml_dtypes.bfloat16)).reshape(k // 32, 32, n)
    amax = np.abs(w).max(1)
    byte = np.clip(np.where(amax > 0, np.frexp(amax)[1] - 1 + 127 - 7, 1), 1, 254)
    scaled = (w * np.exp2(127.0 - byte)[:, None, :]).reshape(k, n).astype(np.float32)
    words = np.ascontiguousarray(scaled.reshape(k // 512, 128, 4, n).transpose(0, 1, 3, 2)).astype(ml_dtypes.float8_e4m3fn).view(np.uint8)
    return words, np.ascontiguousarray(byte.astype(np.uint8).reshape(k // 512, 16, n))


def unpack_weight(words, scales):
    g, p, n, _ = words.shape
    vals = np.ascontiguousarray(words).view(ml_dtypes.float8_e4m3fn).astype(np.float64) * np.repeat(np.exp2(scales.astype(np.float64) - 127.0), 8, axis=1)[..., None]
    return vals.transpose(0, 1, 3, 2).reshape(g * 512, n)


E2M1 = np.array([0.0, 0.5, 1.0, 1.5, 2.0, 3.0, 4.0, 6.0, -0.0, -0.5, -1.0, -1.5, -2.0, -3.0, -4.0, -6.0])


def pack_fp4(w):
    k, n = w.shape
    w = f64(np.asarray(w, np.float32).astype(ml_dtypes.bfloat16)).reshape(k // 32, 32, n)
    amax = np.abs(w).max(1)
    mant, ex = np.frexp(amax / 6.0)
    byte = np.clip(np.where(amax > 0, np.where(mant > 0.5, ex, ex - 1) + 127, 1), 1, 254)
    scaled = (w * np.exp2(127.0 - byte)[:, None, :]).reshape(k, n).astype(np.float32)
    c = np.ascontiguousarray(scaled.reshape(k // 512, 128, 4, n).transpose(0, 1, 3, 2)).astype(ml_dtypes.float4_e2m1fn).view(np.uint8) & 0xF
    words = (c[..., 0::2] | (c[..., 1::2] << 4)).reshape(k // 512, 128, 2 * n)
    return np.ascontiguousarray(words), np.ascontiguousarray(byte.astype(np.uint8).reshape(k // 512, 16, n))


def unpack_fp4(words, scales):
    g, _, n = scales.shape
    words = np.ascontiguousarray(words).reshape(g, 128, n, 2)
    nib = np.empty((g, 128, n, 4), np.uint8)
    nib[..., 0::2] = words & 0xF
    nib[..., 1::2] = words >> 4
    vals = E2M1[nib] * np.repeat(np.exp2(scales.astype(np.float64) - 127.0), 8, axis=1)[..., None]
    return vals.transpose(0, 1, 3, 2).reshape(g * 512, n)


def planes(y):
    n, m = y.shape
    v = y.astype(np.float32).astype(ml_dtypes.bfloat16).astype(np.float64).reshape(n // 32, 32, m)
    top = np.abs(v).max(1)
    byte = np.clip(np.where(top > 0, np.frexp(top)[1] - 1 + 127 - 7, 1), 1, 254)
    codes = (v * np.exp2(127.0 - byte)[:, None, :]).reshape(n, m).astype(np.float32).astype(ml_dtypes.float8_e4m3fn).view(np.uint8)
    words = codes.reshape(n // 512, 128, 4, m).transpose(0, 1, 3, 2)
    return np.ascontiguousarray(words), np.ascontiguousarray(byte.astype(np.uint8).reshape(n // 512, 16, m))


K, T, S, H, W, C, J = 512, 2048, 512, 512, 2048, 512, 512


def setup_inputs():
    n = np.random.standard_normal
    s = mx_kscale(K)[:, None]
    packed_xT = pack_weight(n((K, T)) * s)
    packed_w1 = pack_fp4(n((K, H)) / np.sqrt(K) / s)
    return {
        "x_words": packed_xT[0],
        "x_scales": packed_xT[1],
        "w1_words": packed_w1[0],
        "w1_scales": packed_w1[1],
        "tau": np.random.uniform(0.3, 0.9, (H, 1)).astype(np.float32),
        "gs": (np.random.uniform(0.5, 1.5, (K, 1)) / s).astype(np.float32),
        "tab": n((C, J)).astype(np.float32),
        "offs": striped8(np.random.randint(0, T, (8, S))),
        "n1": striped(np.random.randint(0, S, W)),
        "cand": striped8(np.random.randint(0, T, (8, C))),
        "n2": striped(np.random.randint(0, J, S)),
        "n3": striped(np.random.randint(0, J, S)),
        "n4": striped(np.random.permutation(S)),
    }


def reference(x_words, x_scales, w1_words, w1_scales, tau, gs, tab, offs, n1, cand, n2, n3, n4):
    x_cand = unpack_weight(x_words, x_scales)[np.arange(K)[:, None], runs(cand, K)]
    xq = unpack_weight(x_words, x_scales)[np.arange(K)[:, None], runs(offs, K)]
    y = unpack_fp4(w1_words, w1_scales).T @ xq
    top = y.max(axis=1, keepdims=True)
    ea = np.exp(f64(tau) * (y[:, unstriped(n1)] - top))
    mx = ea.reshape(H, S, 4).max(axis=2)
    mn = ea.reshape(H, S, 4).min(axis=2)
    z = f64(gs) * (3.0 * (y * (mx - mn)))
    s = 0.0625 * ((x_cand.T @ mxq(z, 0, "e4m3")))
    out_0 = s[:, unstriped(n4)] * f64(tab)[:, unstriped(n2)] + f64(tab)[:, unstriped(n3)]
    return (out_0,) + planes(out_0)

@@ -1,0 +1,272 @@
+from contextlib import ExitStack
+
+import concourse.mybir as mybir
+
+K, T, S, H, W, C, J = 512, 2048, 512, 512, 2048, 512, 512
+FLOPS = 2 * K * H * S + 2 * K * C * S
+
+F32 = mybir.dt.float32
+BF16 = mybir.dt.bfloat16
+I32 = mybir.dt.int32
+U32 = mybir.dt.uint32
+U16 = mybir.dt.uint16
+U8 = mybir.dt.uint8
+FP8X4 = mybir.dt.float8_e4m3fn_x4
+FP4X4 = mybir.dt.float4_e2m1fn_x4
+ALU = mybir.AluOpType
+ACT = mybir.ActivationFunctionType
+
+P = 128
+PACK = 4
+MEMBERS = 4
+CHUNK = 64
+N_CHUNKS = S // CHUNK
+GROUP_ENDS = (4, 6, 8)
+HALF = S // 2
+WALK = 4
+
+
+def tile_picked_hcandegpkinda_none_po_kernel(
+    tc, x_words, x_scales, w1_words, w1_scales, tau, gs, tab, offs, n1, cand, n2, n3, n4, out_0, out_1, out_2
+):
+    nc = tc.nc
+    with ExitStack() as ctx:
+        lists = ctx.enter_context(tc.tile_pool(name="lists", bufs=1))
+        keep = ctx.enter_context(tc.tile_pool(name="keep", bufs=1))
+        ring = ctx.enter_context(tc.tile_pool(name="ring", bufs=2))
+        psum = ctx.enter_context(tc.psum_pool(name="psum", bufs=1))
+
+        def load_list(dram, name):
+            tile = lists.tile(list(dram.shape), U16, name=name)
+            nc.sync.dma_start(tile[:], dram)
+            return tile
+
+        def entries(list_tile, first, count):
+            return list_tile[:, first // 16 : (first + count) // 16]
+
+        offs_sb = load_list(offs, "offs_sb")
+        x_codes = keep.tile([P, T], I32, align_bytes=64)
+        nc.scalar.dma_start(x_codes[:], x_words[0].rearrange("p n r -> p (n r)").bitcast(I32))
+        x_scale_rows = keep.tile([P, T], U8, align_bytes=64)
+        nc.sync.dma_start(
+            x_scale_rows[:].bitcast(I32), x_scales[0].bitcast(I32).unsqueeze(1).to_broadcast([16, 8, T // 4])
+        )
+        w_scale_rows = keep.tile([P, H], U8, align_bytes=64)
+        for b in range(4):
+            nc.sync.dma_start(
+                w_scale_rows[b:P:4, :].bitcast(I32),
+                w1_scales[0, b:16:4, :].bitcast(I32).unsqueeze(1).to_broadcast([4, 8, H // 4]),
+            )
+        w_codes = keep.tile([P, 2 * H], U8, align_bytes=64)
+        nc.sync.dma_start(w_codes[:].bitcast(I32), w1_words[0].bitcast(I32))
+        tau_sb = keep.tile([P, PACK], F32)
+        nc.gpsimd.dma_start(tau_sb[:], tau.rearrange("(p t) o -> p (t o)", t=PACK))
+        gs_sb = keep.tile([P, PACK], F32)
+        nc.gpsimd.dma_start(gs_sb[:], gs.rearrange("(p t) o -> p (t o)", t=PACK))
+        cand_sb = load_list(cand, "cand_sb")
+        n1_sb = load_list(n1, "n1_sb")
+        n2_sb = load_list(n2, "n2_sb")
+        n3_sb = load_list(n3, "n3_sb")
+        n4_sb = load_list(n4, "n4_sb")
+
+        minus_tau = keep.tile([P, PACK], F32)
+        nc.scalar.activation(minus_tau[:], tau_sb[:], ACT.Copy, scale=-1.0)
+
+        def place_scale_rows(gathered, name, queue):
+            plane = keep.tile([P, S], U8, name=name, tag=name, align_bytes=64)
+            nc.gpsimd.memset(plane[:], 0)
+            for q in range(4):
+                queue.dma_start(
+                    plane[32 * q : 32 * q + 4, :].bitcast(I32), gathered[32 * q : 32 * q + 32 : 8, :].bitcast(I32)
+                )
+            return plane
+
+        place_bytes = keep.tile([P, S], U8, align_bytes=64)
+        nc.vector.tensor_copy(place_bytes[:], x_scale_rows[:].indirect(offs_sb[:]))
+        place_scales = place_scale_rows(place_bytes, "place_scales", nc.scalar)
+
+        w_scales_dealt = keep.tile([P, H], U8, tag="w_scales_dealt", align_bytes=64)
+        nc.vector.tensor_copy(
+            w_scales_dealt[:].rearrange("p (t m) -> p t m", t=PACK), w_scale_rows[:].rearrange("p (m t) -> p t m", t=PACK)
+        )
+        w_codes_dealt = keep.tile([P, 2 * H], U8, tag="w_codes_dealt", align_bytes=64)
+        nc.scalar.copy(
+            w_codes_dealt[:].bitcast(U16).rearrange("p (t m) -> p t m", t=PACK),
+            w_codes[:].bitcast(U16).rearrange("p (m t) -> p t m", t=PACK),
+        )
+        place_codes = keep.tile([P, S], I32, tag="place_codes", align_bytes=64)
+        nc.vector.tensor_copy(place_codes[:].bitcast(U32), x_codes[:].bitcast(U32).indirect(offs_sb[:]))
+
+        top = keep.tile([P, PACK], F32)
+        bias = keep.tile([P, PACK], F32)
+        y_weighted = keep.tile([P, PACK, S], F32)
+        y = []
+        for t in range(PACK):
+            y_bank = psum.tile([P, S], F32, name=f"y_bank{t}")
+            nc.tensor.matmul_mx(
+                out=y_bank[:],
+                lhsT=w_codes_dealt[:, 2 * P * t : 2 * P * (t + 1)].bitcast(FP4X4),
+                lhsT_scale=w_scales_dealt[:, P * t : P * (t + 1)],
+                rhs=place_codes[:].bitcast(FP8X4),
+                rhs_scale=place_scales[:],
+                start=True,
+                stop=True,
+            )
+            y_t = keep.tile([P, S], F32, name=f"y{t}")
+            nc.vector.tensor_scalar(y_t[:], y_bank[:], 1.0, None, ALU.mult, ALU.max, accum_out=top[:, t : t + 1])
+            nc.gpsimd.tensor_tensor(bias[:, t : t + 1], top[:, t : t + 1], minus_tau[:, t : t + 1], ALU.mult)
+            nc.gpsimd.tensor_scalar(y_weighted[:, t, :], y_t[:], gs_sb[:, t : t + 1], 3.0, ALU.mult, ALU.mult)
+            y.append(y_t)
+
+        def fetch_tab_on_scalar(dst, t, list_tile, h):
+            nc.scalar.activation(dst, tab_sb[t][:].indirect(entries(list_tile, h * HALF, HALF)), ACT.Copy)
+
+        tab_rows = tab.rearrange("(p t) j -> p t j", t=PACK)
+        tab_sb = []
+        for t, tag in enumerate(("place_scales", "w_scales_dealt", "w_codes_dealt", "place_codes")):
+            tile = keep.tile([P, J], F32, name=f"tab{t}", tag=tag, align_bytes=64)
+            nc.sync.dma_start(tile[:], tab_rows[:, t, :])
+            tab_sb.append(tile)
+
+        cand_bytes = keep.tile([P, C], U8, align_bytes=64)
+        nc.vector.tensor_copy(cand_bytes[:], x_scale_rows[:].indirect(cand_sb[:]))
+        cand_codes = keep.tile([P, C], I32, align_bytes=64)
+        nc.vector.tensor_copy(cand_codes[:].bitcast(U32), x_codes[:].bitcast(U32).indirect(cand_sb[:]))
+        cand_bytes_dealt = keep.tile([P, C], U8, align_bytes=64)
+        nc.vector.tensor_copy(
+            cand_bytes_dealt[:].rearrange("p (t m) -> p t m", t=PACK), cand_bytes[:].rearrange("p (m t) -> p t m", t=PACK)
+        )
+        cand_codes_dealt = keep.tile([P, C], I32, align_bytes=64)
+        nc.vector.tensor_copy(
+            cand_codes_dealt[:].rearrange("p (t m) -> p t m", t=PACK), cand_codes[:].rearrange("p (m t) -> p t m", t=PACK)
+        )
+        cand_scales = place_scale_rows(cand_bytes_dealt, "cand_scales", nc.sync)
+
+        z_codes = keep.tile([P, S], I32, align_bytes=64)
+        z_scales = keep.tile([P, S], U8, align_bytes=64)
+        s_banks = [psum.tile([P, S], F32, name=f"s_bank{t}") for t in range(PACK)]
+        s = [keep.tile([P, S], F32, name=f"s{t}") for t in range(PACK)]
+        group_starts = (0,) + GROUP_ENDS[:-1]
+        z_tiles = [
+            keep.tile([P, (end - start) * CHUNK * PACK], BF16, name=f"z{start}", align_bytes=64)
+            for start, end in zip(group_starts, GROUP_ENDS)
+        ]
+
+        ea, upper, lower, most, least, spread = {}, {}, {}, {}, {}, {}
+
+        def fetch_exp(c):
+            ea[c] = keep.tile([P, PACK, CHUNK * MEMBERS], F32, name=f"ea{c}", tag=f"ea{c}")
+            for t in range(PACK):
+                nc.scalar.activation(
+                    ea[c][:, t, :],
+                    y[t][:].indirect(entries(n1_sb, c * CHUNK * MEMBERS, CHUNK * MEMBERS)),
+                    ACT.Exp,
+                    bias=bias[:, t : t + 1],
+                    scale=tau_sb[:, t : t + 1],
+                )
+
+        def pair_up(c, results, op, name):
+            members = ea[c][:].rearrange("p t (j m) -> p (t j) m", m=MEMBERS)
+            results[c] = ring.tile([P, PACK * CHUNK, 2], F32, name=name)
+            nc.vector.tensor_tensor(results[c][:], members[:, :, 0:2], members[:, :, 2:4], op)
+
+        def finish_pairs(c, pairs, results, op, name):
+            results[c] = ring.tile([P, PACK * CHUNK], F32, name=name)
+            nc.vector.tensor_tensor(results[c][:], pairs[c][:, :, 0], pairs[c][:, :, 1], op)
+
+        def subtract(c):
+            spread[c] = keep.tile([P, PACK * CHUNK], F32, name=f"spread{c}", tag=f"spread{c}")
+            nc.vector.tensor_tensor(spread[c][:], most[c][:], least[c][:], ALU.subtract)
+
+        def make_z(c):
+            g = [c < end for end in GROUP_ENDS].index(True)
+            first = (c - group_starts[g]) * CHUNK * PACK
+            nc.vector.tensor_tensor(
+                z_tiles[g][:, first : first + CHUNK * PACK].rearrange("p (a i t) -> p a t i", i=WALK, t=PACK),
+                spread[c][:].rearrange("p (t a i) -> p a t i", t=PACK, i=WALK),
+                y_weighted[:, :, c * CHUNK : (c + 1) * CHUNK].rearrange("p t (a i) -> p a t i", i=WALK),
+                ALU.mult,
+            )
+
+        def score_group(g):
+            cols = slice(group_starts[g] * CHUNK, GROUP_ENDS[g] * CHUNK)
+            nc.vector.quantize_mx(out=z_codes[:, cols].bitcast(FP8X4), scales=z_scales[:, cols], in_=z_tiles[g][:])
+            for t in range(PACK):
+                nc.tensor.matmul_mx(
+                    out=s_banks[t][:, cols],
+                    lhsT=cand_codes_dealt[:, P * t : P * (t + 1)].bitcast(FP8X4),
+                    lhsT_scale=cand_scales[:, P * t : P * (t + 1)],
+                    rhs=z_codes[:, cols].bitcast(FP8X4),
+                    rhs_scale=z_scales[:, cols],
+                    start=True,
+                    stop=True,
+                )
+                nc.scalar.activation(s[t][:, cols], s_banks[t][:, cols], ACT.Copy, scale=0.0625)
+
+        for c in range(N_CHUNKS + 1):
+            if c < N_CHUNKS:
+                fetch_exp(c)
+                pair_up(c, upper, ALU.max, "upper")
+            if c > 0:
+                subtract(c - 1)
+            if c < N_CHUNKS:
+                pair_up(c, lower, ALU.min, "lower")
+            if c > 0:
+                make_z(c - 1)
+            if c < N_CHUNKS:
+                finish_pairs(c, upper, most, ALU.max, "most")
+            if c in GROUP_ENDS:
+                score_group(GROUP_ENDS.index(c))
+            if c < N_CHUNKS:
+                finish_pairs(c, lower, least, ALU.min, "least")
+
+        factor0 = keep.tile([P, PACK, HALF], F32, tag="ea1")
+        for t in range(PACK):
+            fetch_tab_on_scalar(factor0[:, t, :], t, n2_sb, 0)
+        term0 = keep.tile([P, PACK, HALF], F32, tag="ea0")
+        for t in range(PACK):
+            fetch_tab_on_scalar(term0[:, t, :], t, n3_sb, 0)
+        factor1 = keep.tile([P, PACK, HALF], F32, tag=f"ea{N_CHUNKS - 1}")
+        for t in range(PACK):
+            fetch_tab_on_scalar(factor1[:, t, :], t, n2_sb, 1)
+        term1_low = keep.tile([P, 2, HALF], F32, tag=f"spread{N_CHUNKS - 1}")
+        for t in range(2):
+            nc.vector.tensor_copy(term1_low[:, t, :], tab_sb[t][:].indirect(entries(n3_sb, HALF, HALF)))
+
+        out_rows = out_0.rearrange("(p t) j -> p t j", t=PACK)
+        out_words = out_1[0].rearrange("p c r -> p (c r)").bitcast(I32)
+        out_scales = keep.tile([P, S], U8, align_bytes=64)
+
+        def hand_out(h, result, round_engine_copy):
+            cols = slice(h * HALF, (h + 1) * HALF)
+            nc.sync.dma_start(out_rows[:, :, cols], result[:])
+            rounded = keep.tile([P, HALF * PACK], BF16, name=f"rounded{h}", align_bytes=64)
+            round_engine_copy(
+                rounded[:].rearrange("p (a i t) -> p a t i", i=WALK, t=PACK),
+                result[:].rearrange("p t (a i) -> p a t i", i=WALK),
+            )
+            codes = keep.tile([P, HALF], I32, name=f"out_codes{h}", align_bytes=64)
+            nc.vector.quantize_mx(out=codes[:].bitcast(FP8X4), scales=out_scales[:, cols], in_=rounded[:])
+            nc.sync.dma_start(out_words[:, cols], codes[:])
+
+        product0 = keep.tile([P, PACK, HALF], F32)
+        result0 = keep.tile([P, PACK, HALF], F32)
+        picked1 = keep.tile([P, PACK, HALF], F32)
+        product1 = keep.tile([P, PACK, HALF], F32)
+        result1 = keep.tile([P, PACK, HALF], F32)
+        for t in range(PACK):
+            nc.vector.tensor_tensor(product0[:, t, :], s[t][:].indirect(entries(n4_sb, 0, HALF)), factor0[:, t, :], ALU.mult)
+            nc.scalar.activation(picked1[:, t, :], s[t][:].indirect(entries(n4_sb, HALF, HALF)), ACT.Copy)
+            if t % 2 == 1:
+                both = slice(t - 1, t + 1)
+                nc.vector.tensor_tensor(result0[:, both, :], product0[:, both, :], term0[:, both, :], ALU.add)
+        for t in range(2, PACK):
+            fetch_tab_on_scalar(factor0[:, t - 2, :], t, n3_sb, 1)
+        for both, term in ((slice(0, 2), term1_low[:]), (slice(2, 4), factor0[:, 0:2, :])):
+            nc.vector.tensor_tensor(product1[:, both, :], picked1[:, both, :], factor1[:, both, :], ALU.mult)
+            nc.vector.tensor_tensor(result1[:, both, :], product1[:, both, :], term, ALU.add)
+        hand_out(0, result0, nc.scalar.copy)
+        hand_out(1, result1, nc.vector.tensor_copy)
+        for q in range(4):
+            queue = nc.sync if q % 2 == 0 else nc.scalar
+            queue.dma_start(out_2[0, 4 * q : 4 * q + 4, :].bitcast(I32), out_scales[32 * q : 32 * q + 4, :].bitcast(I32))

@@ -19,9 +19,10 @@ ACT = mybir.ActivationFunctionType
 P = 128
 PACK = 4
 MEMBERS = 4
-CHUNK = 64
+CHUNK = 128
 N_CHUNKS = S // CHUNK
-GROUP_ENDS = (4, 6, 8)
+Y_WINDOW = 1024
+WINDOW = 704
 HALF = S // 2
 WALK = 4
 
@@ -44,51 +45,59 @@ def tile_picked_hcandegpkinda_none_po_kernel(
         def entries(list_tile, first, count):
             return list_tile[:, first // 16 : (first + count) // 16]
 
+        def repeated_rows(scales):
+            rows = scales[0].bitcast(I32)
+            return rows.unsqueeze(1).to_broadcast([16, 8, rows.shape[1]])
+
+        tab_rows = tab.rearrange("(p t) j -> p t j", t=PACK)
+        tab_sb = {}
+
+        def load_tab(t, tag):
+            tab_sb[t] = keep.tile([P, WINDOW], F32, name=f"tab{t}", tag=tag, align_bytes=64)
+            nc.sync.dma_start(tab_sb[t][:, :J], tab_rows[:, t, :])
+
         offs_sb = load_list(offs, "offs_sb")
+        x_scale_rows = keep.tile([P, T], U8, align_bytes=64)
+        nc.scalar.dma_start(x_scale_rows[:].bitcast(I32), repeated_rows(x_scales))
+        cand_sb = load_list(cand, "cand_sb")
         x_codes = keep.tile([P, T], I32, align_bytes=64)
         nc.scalar.dma_start(x_codes[:], x_words[0].rearrange("p n r -> p (n r)").bitcast(I32))
-        x_scale_rows = keep.tile([P, T], U8, align_bytes=64)
-        nc.sync.dma_start(
-            x_scale_rows[:].bitcast(I32), x_scales[0].bitcast(I32).unsqueeze(1).to_broadcast([16, 8, T // 4])
-        )
         w_scale_rows = keep.tile([P, H], U8, align_bytes=64)
-        for b in range(4):
-            nc.sync.dma_start(
-                w_scale_rows[b:P:4, :].bitcast(I32),
-                w1_scales[0, b:16:4, :].bitcast(I32).unsqueeze(1).to_broadcast([4, 8, H // 4]),
-            )
+        nc.sync.dma_start(w_scale_rows[:].bitcast(I32), repeated_rows(w1_scales))
+        n2_sb = load_list(n2, "n2_sb")
+        load_tab(0, "tab0")
         w_codes = keep.tile([P, 2 * H], U8, align_bytes=64)
         nc.sync.dma_start(w_codes[:].bitcast(I32), w1_words[0].bitcast(I32))
+        n3_sb = load_list(n3, "n3_sb")
+        n1_sb = load_list(n1, "n1_sb")
+        n4_sb = load_list(n4, "n4_sb")
+        load_tab(1, "tab1")
         tau_sb = keep.tile([P, PACK], F32)
         nc.gpsimd.dma_start(tau_sb[:], tau.rearrange("(p t) o -> p (t o)", t=PACK))
         gs_sb = keep.tile([P, PACK], F32)
         nc.gpsimd.dma_start(gs_sb[:], gs.rearrange("(p t) o -> p (t o)", t=PACK))
-        cand_sb = load_list(cand, "cand_sb")
-        n1_sb = load_list(n1, "n1_sb")
-        n2_sb = load_list(n2, "n2_sb")
-        n3_sb = load_list(n3, "n3_sb")
-        n4_sb = load_list(n4, "n4_sb")
 
-        minus_tau = keep.tile([P, PACK], F32)
-        nc.scalar.activation(minus_tau[:], tau_sb[:], ACT.Copy, scale=-1.0)
-
-        def place_scale_rows(gathered, name, queue):
-            plane = keep.tile([P, S], U8, name=name, tag=name, align_bytes=64)
-            nc.gpsimd.memset(plane[:], 0)
+        def place_scale_rows(spread_rows, name):
+            plane = keep.tile(list(spread_rows.shape), U8, name=name, tag=name, align_bytes=64)
+            nc.vector.memset(plane[:].bitcast(I32), 0)
             for q in range(4):
-                queue.dma_start(
-                    plane[32 * q : 32 * q + 4, :].bitcast(I32), gathered[32 * q : 32 * q + 32 : 8, :].bitcast(I32)
+                nc.sync.dma_start(
+                    plane[32 * q : 32 * q + 4, :].bitcast(I32), spread_rows[32 * q : 32 * q + 32 : 8, :].bitcast(I32)
                 )
             return plane
 
+        def fetch_tab_on_scalar(dst, t, list_tile):
+            nc.scalar.activation(dst, tab_sb[t][:].indirect(list_tile[:]), ACT.Copy)
+
         place_bytes = keep.tile([P, S], U8, align_bytes=64)
         nc.vector.tensor_copy(place_bytes[:], x_scale_rows[:].indirect(offs_sb[:]))
-        place_scales = place_scale_rows(place_bytes, "place_scales", nc.scalar)
-
-        w_scales_dealt = keep.tile([P, H], U8, tag="w_scales_dealt", align_bytes=64)
+        first_rows = keep.tile([P, S + H], U8, align_bytes=64)
         nc.vector.tensor_copy(
-            w_scales_dealt[:].rearrange("p (t m) -> p t m", t=PACK), w_scale_rows[:].rearrange("p (m t) -> p t m", t=PACK)
+            first_rows[:, S:].rearrange("p (t m) -> p t m", t=PACK), w_scale_rows[:].rearrange("p (m t) -> p t m", t=PACK)
         )
+        nc.vector.tensor_copy(first_rows[:, :S].bitcast(I32), place_bytes[:].bitcast(I32))
+        first_scales = place_scale_rows(first_rows, "first_scales")
+
         w_codes_dealt = keep.tile([P, 2 * H], U8, tag="w_codes_dealt", align_bytes=64)
         nc.scalar.copy(
             w_codes_dealt[:].bitcast(U16).rearrange("p (t m) -> p t m", t=PACK),
@@ -97,36 +106,35 @@ def tile_picked_hcandegpkinda_none_po_kernel(
         place_codes = keep.tile([P, S], I32, tag="place_codes", align_bytes=64)
         nc.vector.tensor_copy(place_codes[:].bitcast(U32), x_codes[:].bitcast(U32).indirect(offs_sb[:]))
 
+        factor = keep.tile([P, PACK, S], F32)
+        term_0 = keep.tile([P, S], F32)
+        fetch_tab_on_scalar(factor[:, 0, :], 0, n2_sb)
+        fetch_tab_on_scalar(term_0[:], 0, n3_sb)
+        fetch_tab_on_scalar(factor[:, 1, :], 1, n2_sb)
+
         top = keep.tile([P, PACK], F32)
         bias = keep.tile([P, PACK], F32)
         y_weighted = keep.tile([P, PACK, S], F32)
         y = []
         for t in range(PACK):
-            y_bank = psum.tile([P, S], F32, name=f"y_bank{t}")
+            y_bank = psum.tile([P, S], F32, name=f"y_bank{t}", tag=f"y_bank{t}")
             nc.tensor.matmul_mx(
                 out=y_bank[:],
                 lhsT=w_codes_dealt[:, 2 * P * t : 2 * P * (t + 1)].bitcast(FP4X4),
-                lhsT_scale=w_scales_dealt[:, P * t : P * (t + 1)],
+                lhsT_scale=first_scales[:, S + P * t : S + P * (t + 1)],
                 rhs=place_codes[:].bitcast(FP8X4),
-                rhs_scale=place_scales[:],
+                rhs_scale=first_scales[:, :S],
                 start=True,
                 stop=True,
             )
-            y_t = keep.tile([P, S], F32, name=f"y{t}")
-            nc.vector.tensor_scalar(y_t[:], y_bank[:], 1.0, None, ALU.mult, ALU.max, accum_out=top[:, t : t + 1])
-            nc.gpsimd.tensor_tensor(bias[:, t : t + 1], top[:, t : t + 1], minus_tau[:, t : t + 1], ALU.mult)
-            nc.gpsimd.tensor_scalar(y_weighted[:, t, :], y_t[:], gs_sb[:, t : t + 1], 3.0, ALU.mult, ALU.mult)
+            y_t = keep.tile([P, Y_WINDOW], F32, name=f"y{t}")
+            nc.vector.tensor_scalar(y_t[:, :S], y_bank[:], 1.0, None, ALU.mult, ALU.max, accum_out=top[:, t : t + 1])
+            nc.gpsimd.tensor_scalar(bias[:, t : t + 1], top[:, t : t + 1], tau_sb[:, t : t + 1], -1.0, ALU.mult, ALU.mult)
+            nc.gpsimd.tensor_scalar(y_weighted[:, t, :], y_t[:, :S], gs_sb[:, t : t + 1], 3.0, ALU.mult, ALU.mult)
             y.append(y_t)
 
-        def fetch_tab_on_scalar(dst, t, list_tile, h):
-            nc.scalar.activation(dst, tab_sb[t][:].indirect(entries(list_tile, h * HALF, HALF)), ACT.Copy)
-
-        tab_rows = tab.rearrange("(p t) j -> p t j", t=PACK)
-        tab_sb = []
-        for t, tag in enumerate(("place_scales", "w_scales_dealt", "w_codes_dealt", "place_codes")):
-            tile = keep.tile([P, J], F32, name=f"tab{t}", tag=tag, align_bytes=64)
-            nc.sync.dma_start(tile[:], tab_rows[:, t, :])
-            tab_sb.append(tile)
+        load_tab(2, "w_codes_dealt")
+        load_tab(3, "place_codes")
 
         cand_bytes = keep.tile([P, C], U8, align_bytes=64)
         nc.vector.tensor_copy(cand_bytes[:], x_scale_rows[:].indirect(cand_sb[:]))
@@ -140,108 +148,120 @@ def tile_picked_hcandegpkinda_none_po_kernel(
         nc.vector.tensor_copy(
             cand_codes_dealt[:].rearrange("p (t m) -> p t m", t=PACK), cand_codes[:].rearrange("p (m t) -> p t m", t=PACK)
         )
-        cand_scales = place_scale_rows(cand_bytes_dealt, "cand_scales", nc.sync)
+        cand_scales = place_scale_rows(cand_bytes_dealt, "cand_scales")
 
-        z_codes = keep.tile([P, S], I32, align_bytes=64)
-        z_scales = keep.tile([P, S], U8, align_bytes=64)
-        s_banks = [psum.tile([P, S], F32, name=f"s_bank{t}") for t in range(PACK)]
+        z_codes = keep.tile([P, S], I32, tag="z_codes", align_bytes=64)
+        z_scales = keep.tile([P, S], U8, tag="z_scales", align_bytes=64)
         s = [keep.tile([P, S], F32, name=f"s{t}") for t in range(PACK)]
-        group_starts = (0,) + GROUP_ENDS[:-1]
-        z_tiles = [
-            keep.tile([P, (end - start) * CHUNK * PACK], BF16, name=f"z{start}", align_bytes=64)
-            for start, end in zip(group_starts, GROUP_ENDS)
-        ]
+        early_cols = (N_CHUNKS - 1) * CHUNK
+        z_early = keep.tile([P, early_cols * PACK], BF16, align_bytes=64)
+        z_last = keep.tile([P, CHUNK * PACK], BF16, align_bytes=64)
 
         ea, upper, lower, most, least, spread = {}, {}, {}, {}, {}, {}
 
-        def fetch_exp(c):
-            ea[c] = keep.tile([P, PACK, CHUNK * MEMBERS], F32, name=f"ea{c}", tag=f"ea{c}")
-            for t in range(PACK):
+        def fetch_exp(step):
+            c, u = divmod(step, 2)
+            ea[step] = keep.tile([P, 2, CHUNK * MEMBERS], F32, name=f"ea{step}", tag=f"ea{step}")
+            for t in (2 * u, 2 * u + 1):
                 nc.scalar.activation(
-                    ea[c][:, t, :],
+                    ea[step][:, t % 2, :],
                     y[t][:].indirect(entries(n1_sb, c * CHUNK * MEMBERS, CHUNK * MEMBERS)),
                     ACT.Exp,
                     bias=bias[:, t : t + 1],
                     scale=tau_sb[:, t : t + 1],
                 )
 
-        def pair_up(c, results, op, name):
-            members = ea[c][:].rearrange("p t (j m) -> p (t j) m", m=MEMBERS)
-            results[c] = ring.tile([P, PACK * CHUNK, 2], F32, name=name)
-            nc.vector.tensor_tensor(results[c][:], members[:, :, 0:2], members[:, :, 2:4], op)
+        def pair_up(step, results, op, name):
+            members = ea[step][:].rearrange("p t (j m) -> p (t j) m", m=MEMBERS)
+            results[step] = ring.tile([P, 2 * CHUNK, 2], F32, name=name)
+            nc.vector.tensor_tensor(results[step][:], members[:, :, 0:2], members[:, :, 2:4], op)
 
-        def finish_pairs(c, pairs, results, op, name):
-            results[c] = ring.tile([P, PACK * CHUNK], F32, name=name)
-            nc.vector.tensor_tensor(results[c][:], pairs[c][:, :, 0], pairs[c][:, :, 1], op)
+        def finish_pairs(step, pairs, results, op, name):
+            results[step] = ring.tile([P, 2 * CHUNK], F32, name=name)
+            nc.vector.tensor_tensor(results[step][:], pairs[step][:, :, 0], pairs[step][:, :, 1], op)
 
-        def subtract(c):
-            spread[c] = keep.tile([P, PACK * CHUNK], F32, name=f"spread{c}", tag=f"spread{c}")
-            nc.vector.tensor_tensor(spread[c][:], most[c][:], least[c][:], ALU.subtract)
+        def subtract(step):
+            c, u = divmod(step, 2)
+            if u == 0:
+                spread[c] = ring.tile([P, PACK * CHUNK], F32, name="spread")
+            nc.vector.tensor_tensor(
+                spread[c][:, 2 * CHUNK * u : 2 * CHUNK * (u + 1)], most[step][:], least[step][:], ALU.subtract
+            )
 
         def make_z(c):
-            g = [c < end for end in GROUP_ENDS].index(True)
-            first = (c - group_starts[g]) * CHUNK * PACK
+            target = z_last[:] if c == N_CHUNKS - 1 else z_early[:, c * CHUNK * PACK : (c + 1) * CHUNK * PACK]
             nc.vector.tensor_tensor(
-                z_tiles[g][:, first : first + CHUNK * PACK].rearrange("p (a i t) -> p a t i", i=WALK, t=PACK),
+                target.rearrange("p (a i t) -> p a t i", i=WALK, t=PACK),
                 spread[c][:].rearrange("p (t a i) -> p a t i", t=PACK, i=WALK),
                 y_weighted[:, :, c * CHUNK : (c + 1) * CHUNK].rearrange("p t (a i) -> p a t i", i=WALK),
                 ALU.mult,
             )
 
-        def score_group(g):
-            cols = slice(group_starts[g] * CHUNK, GROUP_ENDS[g] * CHUNK)
-            nc.vector.quantize_mx(out=z_codes[:, cols].bitcast(FP8X4), scales=z_scales[:, cols], in_=z_tiles[g][:])
+        def score(z_tile, first, widths, bank_tag):
+            cols = slice(first, first + sum(widths))
+            nc.vector.quantize_mx(out=z_codes[:, cols].bitcast(FP8X4), scales=z_scales[:, cols], in_=z_tile[:])
             for t in range(PACK):
-                nc.tensor.matmul_mx(
-                    out=s_banks[t][:, cols],
-                    lhsT=cand_codes_dealt[:, P * t : P * (t + 1)].bitcast(FP8X4),
-                    lhsT_scale=cand_scales[:, P * t : P * (t + 1)],
-                    rhs=z_codes[:, cols].bitcast(FP8X4),
-                    rhs_scale=z_scales[:, cols],
-                    start=True,
-                    stop=True,
-                )
-                nc.scalar.activation(s[t][:, cols], s_banks[t][:, cols], ACT.Copy, scale=0.0625)
+                bank = psum.tile([P, sum(widths)], F32, name=f"scores{first}_{t}", tag=f"{bank_tag}{t}")
+                start = 0
+                for width in widths:
+                    moving = slice(first + start, first + start + width)
+                    nc.tensor.matmul_mx(
+                        out=bank[:, start : start + width],
+                        lhsT=cand_codes_dealt[:, P * t : P * (t + 1)].bitcast(FP8X4),
+                        lhsT_scale=cand_scales[:, P * t : P * (t + 1)],
+                        rhs=z_codes[:, moving].bitcast(FP8X4),
+                        rhs_scale=z_scales[:, moving],
+                        start=True,
+                        stop=True,
+                    )
+                    start = start + width
+                nc.scalar.activation(s[t][:, cols], bank[:], ACT.Copy, scale=0.0625)
 
-        for c in range(N_CHUNKS + 1):
-            if c < N_CHUNKS:
-                fetch_exp(c)
-                pair_up(c, upper, ALU.max, "upper")
-            if c > 0:
-                subtract(c - 1)
-            if c < N_CHUNKS:
-                pair_up(c, lower, ALU.min, "lower")
-            if c > 0:
-                make_z(c - 1)
-            if c < N_CHUNKS:
-                finish_pairs(c, upper, most, ALU.max, "most")
-            if c in GROUP_ENDS:
-                score_group(GROUP_ENDS.index(c))
-            if c < N_CHUNKS:
-                finish_pairs(c, lower, least, ALU.min, "least")
+        n_steps = 2 * N_CHUNKS
+        for step in range(n_steps + 1):
+            if step < n_steps:
+                fetch_exp(step)
+                pair_up(step, upper, ALU.max, "upper")
+            if step > 0:
+                subtract(step - 1)
+            if step < n_steps:
+                pair_up(step, lower, ALU.min, "lower")
+            if step > 0 and step % 2 == 0:
+                make_z(step // 2 - 1)
+            if step < n_steps:
+                finish_pairs(step, upper, most, ALU.max, "most")
+            if step == n_steps - 2:
+                score(z_early, 0, (256, 128), "s_bank")
+            if step < n_steps:
+                finish_pairs(step, lower, least, ALU.min, "least")
+        score(z_last, early_cols, (CHUNK,), "y_bank")
 
-        factor0 = keep.tile([P, PACK, HALF], F32, tag="ea1")
-        for t in range(PACK):
-            fetch_tab_on_scalar(factor0[:, t, :], t, n2_sb, 0)
-        term0 = keep.tile([P, PACK, HALF], F32, tag="ea0")
-        for t in range(PACK):
-            fetch_tab_on_scalar(term0[:, t, :], t, n3_sb, 0)
-        factor1 = keep.tile([P, PACK, HALF], F32, tag=f"ea{N_CHUNKS - 1}")
-        for t in range(PACK):
-            fetch_tab_on_scalar(factor1[:, t, :], t, n2_sb, 1)
-        term1_low = keep.tile([P, 2, HALF], F32, tag=f"spread{N_CHUNKS - 1}")
-        for t in range(2):
-            nc.vector.tensor_copy(term1_low[:, t, :], tab_sb[t][:].indirect(entries(n3_sb, HALF, HALF)))
+        for t in range(2, PACK):
+            fetch_tab_on_scalar(factor[:, t, :], t, n2_sb)
+        term_1 = keep.tile([P, S], F32, tag="ea0")
+        fetch_tab_on_scalar(term_1[:], 1, n3_sb)
+        term_high = keep.tile([P, 2, S], F32, tag="z_codes", align_bytes=64)
+        for t in range(2, PACK):
+            fetch_tab_on_scalar(term_high[:, t - 2, :], t, n3_sb)
 
         out_rows = out_0.rearrange("(p t) j -> p t j", t=PACK)
         out_words = out_1[0].rearrange("p c r -> p (c r)").bitcast(I32)
         out_scales = keep.tile([P, S], U8, align_bytes=64)
 
-        def hand_out(h, result, round_engine_copy):
+        def add_terms(h, product):
             cols = slice(h * HALF, (h + 1) * HALF)
-            nc.sync.dma_start(out_rows[:, :, cols], result[:])
+            result = keep.tile([P, PACK, HALF], F32, name=f"result{h}")
+            nc.vector.tensor_tensor(result[:, 0, :], product[:, 0, :], term_0[:, cols], ALU.add)
+            nc.vector.tensor_tensor(result[:, 1, :], product[:, 1, :], term_1[:, cols], ALU.add)
+            nc.sync.dma_start(out_rows[:, 0:2, cols], result[:, 0:2, :])
+            nc.vector.tensor_tensor(result[:, 2:4, :], product[:, 2:4, :], term_high[:, :, cols], ALU.add)
+            nc.sync.dma_start(out_rows[:, 2:4, cols], result[:, 2:4, :])
+            return result
+
+        def hand_out(h, result, copy):
+            cols = slice(h * HALF, (h + 1) * HALF)
             rounded = keep.tile([P, HALF * PACK], BF16, name=f"rounded{h}", align_bytes=64)
-            round_engine_copy(
+            copy(
                 rounded[:].rearrange("p (a i t) -> p a t i", i=WALK, t=PACK),
                 result[:].rearrange("p t (a i) -> p a t i", i=WALK),
             )
@@ -250,21 +270,17 @@ def tile_picked_hcandegpkinda_none_po_kernel(
             nc.sync.dma_start(out_words[:, cols], codes[:])
 
         product0 = keep.tile([P, PACK, HALF], F32)
-        result0 = keep.tile([P, PACK, HALF], F32)
         picked1 = keep.tile([P, PACK, HALF], F32)
         product1 = keep.tile([P, PACK, HALF], F32)
-        result1 = keep.tile([P, PACK, HALF], F32)
         for t in range(PACK):
-            nc.vector.tensor_tensor(product0[:, t, :], s[t][:].indirect(entries(n4_sb, 0, HALF)), factor0[:, t, :], ALU.mult)
+            nc.vector.tensor_tensor(
+                product0[:, t, :], s[t][:].indirect(entries(n4_sb, 0, HALF)), factor[:, t, :HALF], ALU.mult
+            )
             nc.scalar.activation(picked1[:, t, :], s[t][:].indirect(entries(n4_sb, HALF, HALF)), ACT.Copy)
-            if t % 2 == 1:
-                both = slice(t - 1, t + 1)
-                nc.vector.tensor_tensor(result0[:, both, :], product0[:, both, :], term0[:, both, :], ALU.add)
-        for t in range(2, PACK):
-            fetch_tab_on_scalar(factor0[:, t - 2, :], t, n3_sb, 1)
-        for both, term in ((slice(0, 2), term1_low[:]), (slice(2, 4), factor0[:, 0:2, :])):
-            nc.vector.tensor_tensor(product1[:, both, :], picked1[:, both, :], factor1[:, both, :], ALU.mult)
-            nc.vector.tensor_tensor(result1[:, both, :], product1[:, both, :], term, ALU.add)
+        result0 = add_terms(0, product0)
+        for both in (slice(0, 2), slice(2, 4)):
+            nc.vector.tensor_tensor(product1[:, both, :], picked1[:, both, :], factor[:, both, HALF:], ALU.mult)
+        result1 = add_terms(1, product1)
         hand_out(0, result0, nc.scalar.copy)
         hand_out(1, result1, nc.vector.tensor_copy)
         for q in range(4):

@@ -21,10 +21,10 @@ PACK = 4
 MEMBERS = 4
 CHUNK = 128
 N_CHUNKS = S // CHUNK
-Y_WINDOW = 1024
+Y_WINDOW = 2048
 WINDOW = 704
 HALF = S // 2
-WALK = 4
+WALK = 2
 
 
 def tile_picked_hcandegpkinda_none_po_kernel(
@@ -52,65 +52,64 @@ def tile_picked_hcandegpkinda_none_po_kernel(
         tab_rows = tab.rearrange("(p t) j -> p t j", t=PACK)
         tab_sb = {}
 
-        def load_tab(t, tag):
+        def load_tab(t, tag, queue):
             tab_sb[t] = keep.tile([P, WINDOW], F32, name=f"tab{t}", tag=tag, align_bytes=64)
-            nc.sync.dma_start(tab_sb[t][:, :J], tab_rows[:, t, :])
+            queue.dma_start(tab_sb[t][:, :J], tab_rows[:, t, :])
 
         offs_sb = load_list(offs, "offs_sb")
         x_scale_rows = keep.tile([P, T], U8, align_bytes=64)
         nc.scalar.dma_start(x_scale_rows[:].bitcast(I32), repeated_rows(x_scales))
+        tau_sb = keep.tile([P, PACK], F32)
+        nc.sync.dma_start(tau_sb[:], tau.rearrange("(p t) o -> p (t o)", t=PACK))
+        n2_sb = load_list(n2, "n2_sb")
+        w_scale_rows = keep.tile([P, H], U8, align_bytes=64)
+        nc.scalar.dma_start(w_scale_rows[:].bitcast(I32), repeated_rows(w1_scales))
+        n3_sb = load_list(n3, "n3_sb")
+        load_tab(0, "tab0", nc.scalar)
         cand_sb = load_list(cand, "cand_sb")
         x_codes = keep.tile([P, T], I32, align_bytes=64)
         nc.scalar.dma_start(x_codes[:], x_words[0].rearrange("p n r -> p (n r)").bitcast(I32))
-        w_scale_rows = keep.tile([P, H], U8, align_bytes=64)
-        nc.sync.dma_start(w_scale_rows[:].bitcast(I32), repeated_rows(w1_scales))
-        n2_sb = load_list(n2, "n2_sb")
-        load_tab(0, "tab0")
         w_codes = keep.tile([P, 2 * H], U8, align_bytes=64)
-        nc.sync.dma_start(w_codes[:].bitcast(I32), w1_words[0].bitcast(I32))
-        n3_sb = load_list(n3, "n3_sb")
+        nc.gpsimd.dma_start(w_codes[:].bitcast(I32), w1_words[0].bitcast(I32))
         n1_sb = load_list(n1, "n1_sb")
         n4_sb = load_list(n4, "n4_sb")
-        load_tab(1, "tab1")
-        tau_sb = keep.tile([P, PACK], F32)
-        nc.gpsimd.dma_start(tau_sb[:], tau.rearrange("(p t) o -> p (t o)", t=PACK))
+        load_tab(1, "tab1", nc.sync)
         gs_sb = keep.tile([P, PACK], F32)
         nc.gpsimd.dma_start(gs_sb[:], gs.rearrange("(p t) o -> p (t o)", t=PACK))
 
-        def place_scale_rows(spread_rows, name):
-            plane = keep.tile(list(spread_rows.shape), U8, name=name, tag=name, align_bytes=64)
-            nc.vector.memset(plane[:].bitcast(I32), 0)
-            for q in range(4):
-                nc.sync.dma_start(
-                    plane[32 * q : 32 * q + 4, :].bitcast(I32), spread_rows[32 * q : 32 * q + 32 : 8, :].bitcast(I32)
-                )
-            return plane
+        minus_tau = keep.tile([P, PACK], F32)
+        nc.scalar.activation(minus_tau[:], tau_sb[:], ACT.Copy, scale=-1.0)
+
+        def place_scale_rows(plane):
+            for b in range(1, 4):
+                nc.sync.dma_start(plane[b:P:32, :].bitcast(I32), plane[8 * b : P : 32, :].bitcast(I32))
 
         def fetch_tab_on_scalar(dst, t, list_tile):
             nc.scalar.activation(dst, tab_sb[t][:].indirect(list_tile[:]), ACT.Copy)
 
         place_bytes = keep.tile([P, S], U8, align_bytes=64)
         nc.vector.tensor_copy(place_bytes[:], x_scale_rows[:].indirect(offs_sb[:]))
-        first_rows = keep.tile([P, S + H], U8, align_bytes=64)
+        first_scales = keep.tile([P, S + H], U8, align_bytes=64)
         nc.vector.tensor_copy(
-            first_rows[:, S:].rearrange("p (t m) -> p t m", t=PACK), w_scale_rows[:].rearrange("p (m t) -> p t m", t=PACK)
+            first_scales[:, S:].rearrange("p (t m) -> p t m", t=PACK), w_scale_rows[:].rearrange("p (m t) -> p t m", t=PACK)
         )
-        nc.vector.tensor_copy(first_rows[:, :S].bitcast(I32), place_bytes[:].bitcast(I32))
-        first_scales = place_scale_rows(first_rows, "first_scales")
+        nc.vector.tensor_copy(first_scales[:, :S].bitcast(I32), place_bytes[:].bitcast(I32))
+        place_scale_rows(first_scales)
 
+        place_codes = keep.tile([P, S], I32, tag="place_codes", align_bytes=64)
+        nc.vector.tensor_copy(place_codes[:].bitcast(U32), x_codes[:].bitcast(U32).indirect(offs_sb[:]))
+
+        factor = keep.tile([P, PACK, S], F32)
+        term_low = keep.tile([P, 2, S], F32)
+        fetch_tab_on_scalar(factor[:, 0, :], 0, n2_sb)
+        fetch_tab_on_scalar(term_low[:, 0, :], 0, n3_sb)
         w_codes_dealt = keep.tile([P, 2 * H], U8, tag="w_codes_dealt", align_bytes=64)
         nc.scalar.copy(
             w_codes_dealt[:].bitcast(U16).rearrange("p (t m) -> p t m", t=PACK),
             w_codes[:].bitcast(U16).rearrange("p (m t) -> p t m", t=PACK),
         )
-        place_codes = keep.tile([P, S], I32, tag="place_codes", align_bytes=64)
-        nc.vector.tensor_copy(place_codes[:].bitcast(U32), x_codes[:].bitcast(U32).indirect(offs_sb[:]))
-
-        factor = keep.tile([P, PACK, S], F32)
-        term_0 = keep.tile([P, S], F32)
-        fetch_tab_on_scalar(factor[:, 0, :], 0, n2_sb)
-        fetch_tab_on_scalar(term_0[:], 0, n3_sb)
         fetch_tab_on_scalar(factor[:, 1, :], 1, n2_sb)
+        fetch_tab_on_scalar(term_low[:, 1, :], 1, n3_sb)
 
         top = keep.tile([P, PACK], F32)
         bias = keep.tile([P, PACK], F32)
@@ -129,71 +128,80 @@ def tile_picked_hcandegpkinda_none_po_kernel(
             )
             y_t = keep.tile([P, Y_WINDOW], F32, name=f"y{t}")
             nc.vector.tensor_scalar(y_t[:, :S], y_bank[:], 1.0, None, ALU.mult, ALU.max, accum_out=top[:, t : t + 1])
-            nc.gpsimd.tensor_scalar(bias[:, t : t + 1], top[:, t : t + 1], tau_sb[:, t : t + 1], -1.0, ALU.mult, ALU.mult)
+            nc.gpsimd.tensor_tensor(bias[:, t : t + 1], top[:, t : t + 1], minus_tau[:, t : t + 1], ALU.mult)
             nc.gpsimd.tensor_scalar(y_weighted[:, t, :], y_t[:, :S], gs_sb[:, t : t + 1], 3.0, ALU.mult, ALU.mult)
             y.append(y_t)
 
-        load_tab(2, "w_codes_dealt")
-        load_tab(3, "place_codes")
+        load_tab(2, "w_codes_dealt", nc.sync)
+        load_tab(3, "place_codes", nc.sync)
 
         cand_bytes = keep.tile([P, C], U8, align_bytes=64)
         nc.vector.tensor_copy(cand_bytes[:], x_scale_rows[:].indirect(cand_sb[:]))
         cand_codes = keep.tile([P, C], I32, align_bytes=64)
         nc.vector.tensor_copy(cand_codes[:].bitcast(U32), x_codes[:].bitcast(U32).indirect(cand_sb[:]))
-        cand_bytes_dealt = keep.tile([P, C], U8, align_bytes=64)
+        cand_scales = keep.tile([P, C], U8, align_bytes=64)
         nc.vector.tensor_copy(
-            cand_bytes_dealt[:].rearrange("p (t m) -> p t m", t=PACK), cand_bytes[:].rearrange("p (m t) -> p t m", t=PACK)
+            cand_scales[:].rearrange("p (t m) -> p t m", t=PACK), cand_bytes[:].rearrange("p (m t) -> p t m", t=PACK)
         )
         cand_codes_dealt = keep.tile([P, C], I32, align_bytes=64)
         nc.vector.tensor_copy(
-            cand_codes_dealt[:].rearrange("p (t m) -> p t m", t=PACK), cand_codes[:].rearrange("p (m t) -> p t m", t=PACK)
+            cand_codes_dealt[:].rearrange("p (t a i) -> p a t i", t=PACK, i=4),
+            cand_codes[:].rearrange("p (a i t) -> p a t i", t=PACK, i=4),
         )
-        cand_scales = place_scale_rows(cand_bytes_dealt, "cand_scales")
+        place_scale_rows(cand_scales)
 
         z_codes = keep.tile([P, S], I32, tag="z_codes", align_bytes=64)
         z_scales = keep.tile([P, S], U8, tag="z_scales", align_bytes=64)
         s = [keep.tile([P, S], F32, name=f"s{t}") for t in range(PACK)]
         early_cols = (N_CHUNKS - 1) * CHUNK
         z_early = keep.tile([P, early_cols * PACK], BF16, align_bytes=64)
-        z_last = keep.tile([P, CHUNK * PACK], BF16, align_bytes=64)
+        z_last = keep.tile([P, CHUNK * PACK], BF16, tag="z_last", align_bytes=64)
 
+        batches = [(0, 2 * CHUNK, t, 1) for t in range(PACK)]
+        batches = batches + [(2 * CHUNK, CHUNK, t, 2) for t in (0, 2)]
+        batches = batches + [(3 * CHUNK, CHUNK, 0, 2), (3 * CHUNK, CHUNK, 2, 1), (3 * CHUNK, CHUNK, 3, 1)]
         ea, upper, lower, most, least, spread = {}, {}, {}, {}, {}, {}
 
         def fetch_exp(step):
-            c, u = divmod(step, 2)
-            ea[step] = keep.tile([P, 2, CHUNK * MEMBERS], F32, name=f"ea{step}", tag=f"ea{step}")
-            for t in (2 * u, 2 * u + 1):
+            first, width, t0, tiles = batches[step]
+            ea[step] = keep.tile([P, tiles, width * MEMBERS], F32, name=f"ea{step}")
+            for t in range(t0, t0 + tiles):
                 nc.scalar.activation(
-                    ea[step][:, t % 2, :],
-                    y[t][:].indirect(entries(n1_sb, c * CHUNK * MEMBERS, CHUNK * MEMBERS)),
+                    ea[step][:, t - t0, :],
+                    y[t][:].indirect(entries(n1_sb, first * MEMBERS, width * MEMBERS)),
                     ACT.Exp,
                     bias=bias[:, t : t + 1],
                     scale=tau_sb[:, t : t + 1],
                 )
 
         def pair_up(step, results, op, name):
-            members = ea[step][:].rearrange("p t (j m) -> p (t j) m", m=MEMBERS)
-            results[step] = ring.tile([P, 2 * CHUNK, 2], F32, name=name)
-            nc.vector.tensor_tensor(results[step][:], members[:, :, 0:2], members[:, :, 2:4], op)
-
-        def finish_pairs(step, pairs, results, op, name):
-            results[step] = ring.tile([P, 2 * CHUNK], F32, name=name)
-            nc.vector.tensor_tensor(results[step][:], pairs[step][:, :, 0], pairs[step][:, :, 1], op)
-
-        def subtract(step):
-            c, u = divmod(step, 2)
-            if u == 0:
-                spread[c] = ring.tile([P, PACK * CHUNK], F32, name="spread")
+            members = ea[step][:].rearrange("p t (a i m) -> p (t a) i m", i=2, m=MEMBERS)
+            results[step] = ring.tile([P, batches[step][1] * batches[step][3] // 2, 2, 2], F32, name=name)
             nc.vector.tensor_tensor(
-                spread[c][:, 2 * CHUNK * u : 2 * CHUNK * (u + 1)], most[step][:], least[step][:], ALU.subtract
+                results[step][:].rearrange("p a h i -> p a i h"), members[:, :, :, 0:2], members[:, :, :, 2:4], op
             )
 
-        def make_z(c):
-            target = z_last[:] if c == N_CHUNKS - 1 else z_early[:, c * CHUNK * PACK : (c + 1) * CHUNK * PACK]
+        def finish_pairs(step, pairs, results, op, name):
+            results[step] = ring.tile([P, batches[step][1] * batches[step][3]], F32, name=name)
+            nc.vector.tensor_tensor(
+                results[step][:].rearrange("p (a i) -> p a i", i=2), pairs[step][:, :, 0, :], pairs[step][:, :, 1, :], op
+            )
+
+        def subtract(step):
+            first, width, t0, tiles = batches[step]
+            if t0 == 0:
+                spread[first] = keep.tile([P, PACK * width], F32, name=f"spread{first}")
+            nc.vector.tensor_tensor(
+                spread[first][:, t0 * width : (t0 + tiles) * width], most[step][:], least[step][:], ALU.subtract
+            )
+
+        def make_z(step):
+            first, width, t0, tiles = batches[step]
+            target = z_last[:] if first == early_cols else z_early[:, first * PACK : (first + width) * PACK]
             nc.vector.tensor_tensor(
                 target.rearrange("p (a i t) -> p a t i", i=WALK, t=PACK),
-                spread[c][:].rearrange("p (t a i) -> p a t i", t=PACK, i=WALK),
-                y_weighted[:, :, c * CHUNK : (c + 1) * CHUNK].rearrange("p t (a i) -> p a t i", i=WALK),
+                spread[first][:].rearrange("p (t a i) -> p a t i", t=PACK, i=WALK),
+                y_weighted[:, :, first : first + width].rearrange("p t (a i) -> p a t i", i=WALK),
                 ALU.mult,
             )
 
@@ -217,7 +225,7 @@ def tile_picked_hcandegpkinda_none_po_kernel(
                     start = start + width
                 nc.scalar.activation(s[t][:, cols], bank[:], ACT.Copy, scale=0.0625)
 
-        n_steps = 2 * N_CHUNKS
+        n_steps = len(batches)
         for step in range(n_steps + 1):
             if step < n_steps:
                 fetch_exp(step)
@@ -226,11 +234,11 @@ def tile_picked_hcandegpkinda_none_po_kernel(
                 subtract(step - 1)
             if step < n_steps:
                 pair_up(step, lower, ALU.min, "lower")
-            if step > 0 and step % 2 == 0:
-                make_z(step // 2 - 1)
+            if step > 0 and sum(batches[step - 1][2:]) == PACK:
+                make_z(step - 1)
             if step < n_steps:
                 finish_pairs(step, upper, most, ALU.max, "most")
-            if step == n_steps - 2:
+            if step > 0 and batches[step - 1] == (2 * CHUNK, CHUNK, 2, 2):
                 score(z_early, 0, (256, 128), "s_bank")
             if step < n_steps:
                 finish_pairs(step, lower, least, ALU.min, "least")
@@ -238,11 +246,10 @@ def tile_picked_hcandegpkinda_none_po_kernel(
 
         for t in range(2, PACK):
             fetch_tab_on_scalar(factor[:, t, :], t, n2_sb)
-        term_1 = keep.tile([P, S], F32, tag="ea0")
-        fetch_tab_on_scalar(term_1[:], 1, n3_sb)
-        term_high = keep.tile([P, 2, S], F32, tag="z_codes", align_bytes=64)
-        for t in range(2, PACK):
-            fetch_tab_on_scalar(term_high[:, t - 2, :], t, n3_sb)
+        term_3 = keep.tile([P, S], F32, tag="z_last", align_bytes=64)
+        nc.vector.tensor_copy(term_3[:], tab_sb[3][:].indirect(n3_sb[:]))
+        term_2 = keep.tile([P, S], F32)
+        fetch_tab_on_scalar(term_2[:], 2, n3_sb)
 
         out_rows = out_0.rearrange("(p t) j -> p t j", t=PACK)
         out_words = out_1[0].rearrange("p c r -> p (c r)").bitcast(I32)
@@ -251,38 +258,48 @@ def tile_picked_hcandegpkinda_none_po_kernel(
         def add_terms(h, product):
             cols = slice(h * HALF, (h + 1) * HALF)
             result = keep.tile([P, PACK, HALF], F32, name=f"result{h}")
-            nc.vector.tensor_tensor(result[:, 0, :], product[:, 0, :], term_0[:, cols], ALU.add)
-            nc.vector.tensor_tensor(result[:, 1, :], product[:, 1, :], term_1[:, cols], ALU.add)
+            nc.vector.tensor_tensor(result[:, 0:2, :], product[:, 0:2, :], term_low[:, :, cols], ALU.add)
             nc.sync.dma_start(out_rows[:, 0:2, cols], result[:, 0:2, :])
-            nc.vector.tensor_tensor(result[:, 2:4, :], product[:, 2:4, :], term_high[:, :, cols], ALU.add)
+            nc.vector.tensor_tensor(result[:, 3, :], product[:, 3, :], term_3[:, cols], ALU.add)
+            nc.vector.tensor_tensor(result[:, 2, :], product[:, 2, :], term_2[:, cols], ALU.add)
             nc.sync.dma_start(out_rows[:, 2:4, cols], result[:, 2:4, :])
             return result
 
-        def hand_out(h, result, copy):
+        def hand_out(h, result, vector_cols):
             cols = slice(h * HALF, (h + 1) * HALF)
             rounded = keep.tile([P, HALF * PACK], BF16, name=f"rounded{h}", align_bytes=64)
-            copy(
-                rounded[:].rearrange("p (a i t) -> p a t i", i=WALK, t=PACK),
-                result[:].rearrange("p t (a i) -> p a t i", i=WALK),
-            )
+            for copy, first, end in ((nc.vector.tensor_copy, 0, vector_cols), (nc.scalar.copy, vector_cols, HALF)):
+                if end > first:
+                    copy(
+                        rounded[:, first * PACK : end * PACK].rearrange("p (a i t) -> p a t i", i=WALK, t=PACK),
+                        result[:, :, first:end].rearrange("p t (a i) -> p a t i", i=WALK),
+                    )
             codes = keep.tile([P, HALF], I32, name=f"out_codes{h}", align_bytes=64)
             nc.vector.quantize_mx(out=codes[:].bitcast(FP8X4), scales=out_scales[:, cols], in_=rounded[:])
             nc.sync.dma_start(out_words[:, cols], codes[:])
 
+        def pick_on_scalar(dst, t, h):
+            nc.scalar.activation(dst, s[t][:].indirect(entries(n4_sb, h * HALF, HALF)), ACT.Copy)
+
         product0 = keep.tile([P, PACK, HALF], F32)
+        picked0 = keep.tile([P, 2, HALF], F32)
         picked1 = keep.tile([P, PACK, HALF], F32)
         product1 = keep.tile([P, PACK, HALF], F32)
-        for t in range(PACK):
+        for t in range(2):
             nc.vector.tensor_tensor(
                 product0[:, t, :], s[t][:].indirect(entries(n4_sb, 0, HALF)), factor[:, t, :HALF], ALU.mult
             )
-            nc.scalar.activation(picked1[:, t, :], s[t][:].indirect(entries(n4_sb, HALF, HALF)), ACT.Copy)
+        for t in range(2, PACK):
+            pick_on_scalar(picked0[:, t - 2, :], t, 0)
+        nc.vector.tensor_tensor(product0[:, 2:4, :], picked0[:], factor[:, 2:4, :HALF], ALU.mult)
+        for t in range(PACK):
+            pick_on_scalar(picked1[:, t, :], t, 1)
         result0 = add_terms(0, product0)
         for both in (slice(0, 2), slice(2, 4)):
             nc.vector.tensor_tensor(product1[:, both, :], picked1[:, both, :], factor[:, both, HALF:], ALU.mult)
         result1 = add_terms(1, product1)
-        hand_out(0, result0, nc.scalar.copy)
-        hand_out(1, result1, nc.vector.tensor_copy)
+        hand_out(0, result0, 0)
+        hand_out(1, result1, 176)
         for q in range(4):
             queue = nc.sync if q % 2 == 0 else nc.scalar
             queue.dma_start(out_2[0, 4 * q : 4 * q + 4, :].bitcast(I32), out_scales[32 * q : 32 * q + 4, :].bitcast(I32))

@@ -2,7 +2,7 @@ from contextlib import ExitStack
 
 import concourse.mybir as mybir
 
-K, T, S, H, W, C, J = 512, 2048, 512, 512, 2048, 512, 512
+K, T, S, H, C, J = 512, 2048, 512, 512, 512, 512
 FLOPS = 2 * K * H * S + 2 * K * C * S
 
 F32 = mybir.dt.float32
@@ -18,13 +18,17 @@ ACT = mybir.ActivationFunctionType
 
 P = 128
 PACK = 4
+SCALE_ROWS = 16
+SCALE_STEP = P // SCALE_ROWS
+QUADRANT = 32
 MEMBERS = 4
-CHUNK = 128
-N_CHUNKS = S // CHUNK
-Y_WINDOW = 2048
-WINDOW = 704
 HALF = S // 2
-WALK = 2
+QUARTER = S // 4
+EARLY = S - QUARTER
+Y_WINDOW = 2048
+TAB_WINDOW = 704
+PAIR = 2
+ROUNDED_ON_VECTOR = 176
 
 
 def tile_picked_hcandegpkinda_none_po_kernel(
@@ -45,25 +49,32 @@ def tile_picked_hcandegpkinda_none_po_kernel(
         def entries(list_tile, first, count):
             return list_tile[:, first // 16 : (first + count) // 16]
 
-        def repeated_rows(scales):
-            rows = scales[0].bitcast(I32)
-            return rows.unsqueeze(1).to_broadcast([16, 8, rows.shape[1]])
-
         tab_rows = tab.rearrange("(p t) j -> p t j", t=PACK)
         tab_sb = {}
 
         def load_tab(t, tag, queue):
-            tab_sb[t] = keep.tile([P, WINDOW], F32, name=f"tab{t}", tag=tag, align_bytes=64)
+            tab_sb[t] = keep.tile([P, TAB_WINDOW], F32, name=f"tab{t}", tag=tag, align_bytes=64)
             queue.dma_start(tab_sb[t][:, :J], tab_rows[:, t, :])
 
+        def place_scale_rows(plane):
+            for b in range(1, PACK):
+                nc.sync.dma_start(plane[b:P:QUADRANT, :].bitcast(I32), plane[SCALE_STEP * b : P : QUADRANT, :].bitcast(I32))
+
+        def fetch_tab_on_scalar(dst, t, list_tile):
+            nc.scalar.activation(dst, tab_sb[t][:].indirect(list_tile[:]), ACT.Copy)
+
         offs_sb = load_list(offs, "offs_sb")
-        x_scale_rows = keep.tile([P, T], U8, align_bytes=64)
-        nc.scalar.dma_start(x_scale_rows[:].bitcast(I32), repeated_rows(x_scales))
         tau_sb = keep.tile([P, PACK], F32)
-        nc.sync.dma_start(tau_sb[:], tau.rearrange("(p t) o -> p (t o)", t=PACK))
+        nc.scalar.dma_start(tau_sb[:], tau.rearrange("(p t) o -> p (t o)", t=PACK))
+        x_scale_rows = keep.tile([P, T], U8, align_bytes=64)
+        nc.vector.memset(x_scale_rows[:].bitcast(I32), 0)
+        nc.scalar.dma_start(x_scale_rows[0:P:SCALE_STEP, :].bitcast(I32), x_scales[0].bitcast(I32))
         n2_sb = load_list(n2, "n2_sb")
-        w_scale_rows = keep.tile([P, H], U8, align_bytes=64)
-        nc.scalar.dma_start(w_scale_rows[:].bitcast(I32), repeated_rows(w1_scales))
+        w_scale_rows = keep.tile([P, H], U8, tag="w_scale_rows", align_bytes=64)
+        nc.scalar.dma_start(
+            w_scale_rows[:].bitcast(I32),
+            w1_scales[0].bitcast(I32).unsqueeze(1).to_broadcast([SCALE_ROWS, SCALE_STEP, H // 4]),
+        )
         n3_sb = load_list(n3, "n3_sb")
         load_tab(0, "tab0", nc.scalar)
         cand_sb = load_list(cand, "cand_sb")
@@ -73,28 +84,22 @@ def tile_picked_hcandegpkinda_none_po_kernel(
         nc.gpsimd.dma_start(w_codes[:].bitcast(I32), w1_words[0].bitcast(I32))
         n1_sb = load_list(n1, "n1_sb")
         n4_sb = load_list(n4, "n4_sb")
-        load_tab(1, "tab1", nc.sync)
         gs_sb = keep.tile([P, PACK], F32)
         nc.gpsimd.dma_start(gs_sb[:], gs.rearrange("(p t) o -> p (t o)", t=PACK))
 
         minus_tau = keep.tile([P, PACK], F32)
         nc.scalar.activation(minus_tau[:], tau_sb[:], ACT.Copy, scale=-1.0)
 
-        def place_scale_rows(plane):
-            for b in range(1, 4):
-                nc.sync.dma_start(plane[b:P:32, :].bitcast(I32), plane[8 * b : P : 32, :].bitcast(I32))
-
-        def fetch_tab_on_scalar(dst, t, list_tile):
-            nc.scalar.activation(dst, tab_sb[t][:].indirect(list_tile[:]), ACT.Copy)
-
         place_bytes = keep.tile([P, S], U8, align_bytes=64)
         nc.vector.tensor_copy(place_bytes[:], x_scale_rows[:].indirect(offs_sb[:]))
         first_scales = keep.tile([P, S + H], U8, align_bytes=64)
-        nc.vector.tensor_copy(
-            first_scales[:, S:].rearrange("p (t m) -> p t m", t=PACK), w_scale_rows[:].rearrange("p (m t) -> p t m", t=PACK)
-        )
         nc.vector.tensor_copy(first_scales[:, :S].bitcast(I32), place_bytes[:].bitcast(I32))
+        nc.vector.tensor_copy(
+            first_scales[:, S:].rearrange("p (t m) -> p t m", t=PACK),
+            w_scale_rows[:].rearrange("p (m t) -> p t m", t=PACK),
+        )
         place_scale_rows(first_scales)
+        load_tab(1, "w_scale_rows", nc.sync)
 
         place_codes = keep.tile([P, S], I32, tag="place_codes", align_bytes=64)
         nc.vector.tensor_copy(place_codes[:].bitcast(U32), x_codes[:].bitcast(U32).indirect(offs_sb[:]))
@@ -150,17 +155,20 @@ def tile_picked_hcandegpkinda_none_po_kernel(
         )
         place_scale_rows(cand_scales)
 
-        z_codes = keep.tile([P, S], I32, tag="z_codes", align_bytes=64)
-        z_scales = keep.tile([P, S], U8, tag="z_scales", align_bytes=64)
+        z_codes = keep.tile([P, S], I32, align_bytes=64)
+        z_scales = keep.tile([P, S], U8, align_bytes=64)
         s = [keep.tile([P, S], F32, name=f"s{t}") for t in range(PACK)]
-        early_cols = (N_CHUNKS - 1) * CHUNK
-        z_early = keep.tile([P, early_cols * PACK], BF16, align_bytes=64)
-        z_last = keep.tile([P, CHUNK * PACK], BF16, tag="z_last", align_bytes=64)
+        z_early = keep.tile([P, EARLY * PACK], BF16, align_bytes=64)
+        z_last = keep.tile([P, QUARTER * PACK], BF16, tag="z_last", align_bytes=64)
 
-        batches = [(0, 2 * CHUNK, t, 1) for t in range(PACK)]
-        batches = batches + [(2 * CHUNK, CHUNK, t, 2) for t in (0, 2)]
-        batches = batches + [(3 * CHUNK, CHUNK, 0, 2), (3 * CHUNK, CHUNK, 2, 1), (3 * CHUNK, CHUNK, 3, 1)]
+        batches = [(0, HALF, t, 1) for t in range(PACK)]
+        batches = batches + [(first, QUARTER, t, 2) for first in (HALF, EARLY) for t in (0, 2)]
+        batch_values = HALF
         ea, upper, lower, most, least, spread = {}, {}, {}, {}, {}, {}
+
+        def ends_columns(step):
+            first, width, t0, tiles = batches[step]
+            return t0 + tiles == PACK
 
         def fetch_exp(step):
             first, width, t0, tiles = batches[step]
@@ -175,16 +183,19 @@ def tile_picked_hcandegpkinda_none_po_kernel(
                 )
 
         def pair_up(step, results, op, name):
-            members = ea[step][:].rearrange("p t (a i m) -> p (t a) i m", i=2, m=MEMBERS)
-            results[step] = ring.tile([P, batches[step][1] * batches[step][3] // 2, 2, 2], F32, name=name)
+            members = ea[step][:].rearrange("p t (a i m) -> p (t a) i m", i=PAIR, m=MEMBERS)
+            results[step] = ring.tile([P, batch_values // PAIR, 2, PAIR], F32, name=name)
             nc.vector.tensor_tensor(
                 results[step][:].rearrange("p a h i -> p a i h"), members[:, :, :, 0:2], members[:, :, :, 2:4], op
             )
 
         def finish_pairs(step, pairs, results, op, name):
-            results[step] = ring.tile([P, batches[step][1] * batches[step][3]], F32, name=name)
+            results[step] = ring.tile([P, batch_values], F32, name=name)
             nc.vector.tensor_tensor(
-                results[step][:].rearrange("p (a i) -> p a i", i=2), pairs[step][:, :, 0, :], pairs[step][:, :, 1, :], op
+                results[step][:].rearrange("p (a i) -> p a i", i=PAIR),
+                pairs[step][:, :, 0, :],
+                pairs[step][:, :, 1, :],
+                op,
             )
 
         def subtract(step):
@@ -197,11 +208,11 @@ def tile_picked_hcandegpkinda_none_po_kernel(
 
         def make_z(step):
             first, width, t0, tiles = batches[step]
-            target = z_last[:] if first == early_cols else z_early[:, first * PACK : (first + width) * PACK]
+            target = z_last[:] if first == EARLY else z_early[:, first * PACK : (first + width) * PACK]
             nc.vector.tensor_tensor(
-                target.rearrange("p (a i t) -> p a t i", i=WALK, t=PACK),
-                spread[first][:].rearrange("p (t a i) -> p a t i", t=PACK, i=WALK),
-                y_weighted[:, :, first : first + width].rearrange("p t (a i) -> p a t i", i=WALK),
+                target.rearrange("p (a i t) -> p a t i", i=PAIR, t=PACK),
+                spread[first][:].rearrange("p (t a i) -> p a t i", t=PACK, i=PAIR),
+                y_weighted[:, :, first : first + width].rearrange("p t (a i) -> p a t i", i=PAIR),
                 ALU.mult,
             )
 
@@ -234,15 +245,15 @@ def tile_picked_hcandegpkinda_none_po_kernel(
                 subtract(step - 1)
             if step < n_steps:
                 pair_up(step, lower, ALU.min, "lower")
-            if step > 0 and sum(batches[step - 1][2:]) == PACK:
+            if step > 0 and ends_columns(step - 1):
                 make_z(step - 1)
             if step < n_steps:
                 finish_pairs(step, upper, most, ALU.max, "most")
-            if step > 0 and batches[step - 1] == (2 * CHUNK, CHUNK, 2, 2):
-                score(z_early, 0, (256, 128), "s_bank")
+            if step > 0 and ends_columns(step - 1) and batches[step - 1][0] == HALF:
+                score(z_early, 0, (HALF, QUARTER), "s_bank")
             if step < n_steps:
                 finish_pairs(step, lower, least, ALU.min, "least")
-        score(z_last, early_cols, (CHUNK,), "y_bank")
+        score(z_last, EARLY, (QUARTER,), "y_bank")
 
         for t in range(2, PACK):
             fetch_tab_on_scalar(factor[:, t, :], t, n2_sb)
@@ -255,6 +266,9 @@ def tile_picked_hcandegpkinda_none_po_kernel(
         out_words = out_1[0].rearrange("p c r -> p (c r)").bitcast(I32)
         out_scales = keep.tile([P, S], U8, align_bytes=64)
 
+        def pick_on_scalar(dst, t, h):
+            nc.scalar.activation(dst, s[t][:].indirect(entries(n4_sb, h * HALF, HALF)), ACT.Copy)
+
         def add_terms(h, product):
             cols = slice(h * HALF, (h + 1) * HALF)
             result = keep.tile([P, PACK, HALF], F32, name=f"result{h}")
@@ -265,21 +279,17 @@ def tile_picked_hcandegpkinda_none_po_kernel(
             nc.sync.dma_start(out_rows[:, 2:4, cols], result[:, 2:4, :])
             return result
 
-        def hand_out(h, result, vector_cols):
+        def hand_out(h, result, shares):
             cols = slice(h * HALF, (h + 1) * HALF)
             rounded = keep.tile([P, HALF * PACK], BF16, name=f"rounded{h}", align_bytes=64)
-            for copy, first, end in ((nc.vector.tensor_copy, 0, vector_cols), (nc.scalar.copy, vector_cols, HALF)):
-                if end > first:
-                    copy(
-                        rounded[:, first * PACK : end * PACK].rearrange("p (a i t) -> p a t i", i=WALK, t=PACK),
-                        result[:, :, first:end].rearrange("p t (a i) -> p a t i", i=WALK),
-                    )
+            for copy, first, end in shares:
+                copy(
+                    rounded[:, first * PACK : end * PACK].rearrange("p (a i t) -> p a t i", i=PAIR, t=PACK),
+                    result[:, :, first:end].rearrange("p t (a i) -> p a t i", i=PAIR),
+                )
             codes = keep.tile([P, HALF], I32, name=f"out_codes{h}", align_bytes=64)
             nc.vector.quantize_mx(out=codes[:].bitcast(FP8X4), scales=out_scales[:, cols], in_=rounded[:])
             nc.sync.dma_start(out_words[:, cols], codes[:])
-
-        def pick_on_scalar(dst, t, h):
-            nc.scalar.activation(dst, s[t][:].indirect(entries(n4_sb, h * HALF, HALF)), ACT.Copy)
 
         product0 = keep.tile([P, PACK, HALF], F32)
         picked0 = keep.tile([P, 2, HALF], F32)
@@ -298,8 +308,12 @@ def tile_picked_hcandegpkinda_none_po_kernel(
         for both in (slice(0, 2), slice(2, 4)):
             nc.vector.tensor_tensor(product1[:, both, :], picked1[:, both, :], factor[:, both, HALF:], ALU.mult)
         result1 = add_terms(1, product1)
-        hand_out(0, result0, 0)
-        hand_out(1, result1, 176)
-        for q in range(4):
+        hand_out(0, result0, [(nc.scalar.copy, 0, HALF)])
+        hand_out(1, result1, [(nc.vector.tensor_copy, 0, ROUNDED_ON_VECTOR), (nc.scalar.copy, ROUNDED_ON_VECTOR, HALF)])
+
+        for q in range(P // QUADRANT):
             queue = nc.sync if q % 2 == 0 else nc.scalar
-            queue.dma_start(out_2[0, 4 * q : 4 * q + 4, :].bitcast(I32), out_scales[32 * q : 32 * q + 4, :].bitcast(I32))
+            queue.dma_start(
+                out_2[0, PACK * q : PACK * (q + 1), :].bitcast(I32),
+                out_scales[QUADRANT * q : QUADRANT * q + PACK, :].bitcast(I32),
+            )

from contextlib import ExitStack

import concourse.mybir as mybir

K, T, S, H, C, J = 512, 2048, 512, 512, 512, 512
FLOPS = 2 * K * H * S + 2 * K * C * S

F32 = mybir.dt.float32
BF16 = mybir.dt.bfloat16
I32 = mybir.dt.int32
U32 = mybir.dt.uint32
U16 = mybir.dt.uint16
U8 = mybir.dt.uint8
FP8X4 = mybir.dt.float8_e4m3fn_x4
FP4X4 = mybir.dt.float4_e2m1fn_x4
ALU = mybir.AluOpType
ACT = mybir.ActivationFunctionType

P = 128
PACK = 4
SCALE_ROWS = 16
SCALE_STEP = P // SCALE_ROWS
QUADRANT = 32
MEMBERS = 4
HALF = S // 2
QUARTER = S // 4
EARLY = S - QUARTER
Y_WINDOW = 2048
TAB_WINDOW = 704
PAIR = 2
ROUNDED_ON_VECTOR = 176


def tile_picked_hcandegpkinda_none_po_kernel(
    tc, x_words, x_scales, w1_words, w1_scales, tau, gs, tab, offs, n1, cand, n2, n3, n4, out_0, out_1, out_2
):
    nc = tc.nc
    with ExitStack() as ctx:
        lists = ctx.enter_context(tc.tile_pool(name="lists", bufs=1))
        keep = ctx.enter_context(tc.tile_pool(name="keep", bufs=1))
        ring = ctx.enter_context(tc.tile_pool(name="ring", bufs=2))
        psum = ctx.enter_context(tc.psum_pool(name="psum", bufs=1))

        def load_list(dram, name):
            tile = lists.tile(list(dram.shape), U16, name=name)
            nc.sync.dma_start(tile[:], dram)
            return tile

        def entries(list_tile, first, count):
            return list_tile[:, first // 16 : (first + count) // 16]

        tab_rows = tab.rearrange("(p t) j -> p t j", t=PACK)
        tab_sb = {}

        def load_tab(t, tag, queue):
            tab_sb[t] = keep.tile([P, TAB_WINDOW], F32, name=f"tab{t}", tag=tag, align_bytes=64)
            queue.dma_start(tab_sb[t][:, :J], tab_rows[:, t, :])

        def place_scale_rows(plane):
            for b in range(1, PACK):
                nc.sync.dma_start(plane[b:P:QUADRANT, :].bitcast(I32), plane[SCALE_STEP * b : P : QUADRANT, :].bitcast(I32))

        def fetch_tab_on_scalar(dst, t, list_tile):
            nc.scalar.activation(dst, tab_sb[t][:].indirect(list_tile[:]), ACT.Copy)

        offs_sb = load_list(offs, "offs_sb")
        tau_sb = keep.tile([P, PACK], F32)
        nc.scalar.dma_start(tau_sb[:], tau.rearrange("(p t) o -> p (t o)", t=PACK))
        x_scale_rows = keep.tile([P, T], U8, align_bytes=64)
        nc.vector.memset(x_scale_rows[:].bitcast(I32), 0)
        nc.scalar.dma_start(x_scale_rows[0:P:SCALE_STEP, :].bitcast(I32), x_scales[0].bitcast(I32))
        n2_sb = load_list(n2, "n2_sb")
        w_scale_rows = keep.tile([P, H], U8, tag="w_scale_rows", align_bytes=64)
        nc.scalar.dma_start(
            w_scale_rows[:].bitcast(I32),
            w1_scales[0].bitcast(I32).unsqueeze(1).to_broadcast([SCALE_ROWS, SCALE_STEP, H // 4]),
        )
        n3_sb = load_list(n3, "n3_sb")
        load_tab(0, "tab0", nc.scalar)
        cand_sb = load_list(cand, "cand_sb")
        x_codes = keep.tile([P, T], I32, align_bytes=64)
        nc.scalar.dma_start(x_codes[:], x_words[0].rearrange("p n r -> p (n r)").bitcast(I32))
        w_codes = keep.tile([P, 2 * H], U8, align_bytes=64)
        nc.gpsimd.dma_start(w_codes[:].bitcast(I32), w1_words[0].bitcast(I32))
        n1_sb = load_list(n1, "n1_sb")
        n4_sb = load_list(n4, "n4_sb")
        gs_sb = keep.tile([P, PACK], F32)
        nc.gpsimd.dma_start(gs_sb[:], gs.rearrange("(p t) o -> p (t o)", t=PACK))

        minus_tau = keep.tile([P, PACK], F32)
        nc.scalar.activation(minus_tau[:], tau_sb[:], ACT.Copy, scale=-1.0)

        place_bytes = keep.tile([P, S], U8, align_bytes=64)
        nc.vector.tensor_copy(place_bytes[:], x_scale_rows[:].indirect(offs_sb[:]))
        first_scales = keep.tile([P, S + H], U8, align_bytes=64)
        nc.vector.tensor_copy(first_scales[:, :S].bitcast(I32), place_bytes[:].bitcast(I32))
        nc.vector.tensor_copy(
            first_scales[:, S:].rearrange("p (t m) -> p t m", t=PACK),
            w_scale_rows[:].rearrange("p (m t) -> p t m", t=PACK),
        )
        place_scale_rows(first_scales)
        load_tab(1, "w_scale_rows", nc.sync)

        place_codes = keep.tile([P, S], I32, tag="place_codes", align_bytes=64)
        nc.vector.tensor_copy(place_codes[:].bitcast(U32), x_codes[:].bitcast(U32).indirect(offs_sb[:]))

        factor = keep.tile([P, PACK, S], F32)
        term_low = keep.tile([P, 2, S], F32)
        fetch_tab_on_scalar(factor[:, 0, :], 0, n2_sb)
        fetch_tab_on_scalar(term_low[:, 0, :], 0, n3_sb)
        w_codes_dealt = keep.tile([P, 2 * H], U8, tag="w_codes_dealt", align_bytes=64)
        nc.scalar.copy(
            w_codes_dealt[:].bitcast(U16).rearrange("p (t m) -> p t m", t=PACK),
            w_codes[:].bitcast(U16).rearrange("p (m t) -> p t m", t=PACK),
        )
        fetch_tab_on_scalar(factor[:, 1, :], 1, n2_sb)
        fetch_tab_on_scalar(term_low[:, 1, :], 1, n3_sb)

        top = keep.tile([P, PACK], F32)
        bias = keep.tile([P, PACK], F32)
        y_weighted = keep.tile([P, PACK, S], F32)
        y = []
        for t in range(PACK):
            y_bank = psum.tile([P, S], F32, name=f"y_bank{t}", tag=f"y_bank{t}")
            nc.tensor.matmul_mx(
                out=y_bank[:],
                lhsT=w_codes_dealt[:, 2 * P * t : 2 * P * (t + 1)].bitcast(FP4X4),
                lhsT_scale=first_scales[:, S + P * t : S + P * (t + 1)],
                rhs=place_codes[:].bitcast(FP8X4),
                rhs_scale=first_scales[:, :S],
                start=True,
                stop=True,
            )
            y_t = keep.tile([P, Y_WINDOW], F32, name=f"y{t}")
            nc.vector.tensor_scalar(y_t[:, :S], y_bank[:], 1.0, None, ALU.mult, ALU.max, accum_out=top[:, t : t + 1])
            nc.gpsimd.tensor_tensor(bias[:, t : t + 1], top[:, t : t + 1], minus_tau[:, t : t + 1], ALU.mult)
            nc.gpsimd.tensor_scalar(y_weighted[:, t, :], y_t[:, :S], gs_sb[:, t : t + 1], 3.0, ALU.mult, ALU.mult)
            y.append(y_t)

        load_tab(2, "w_codes_dealt", nc.sync)
        load_tab(3, "place_codes", nc.sync)

        cand_bytes = keep.tile([P, C], U8, align_bytes=64)
        nc.vector.tensor_copy(cand_bytes[:], x_scale_rows[:].indirect(cand_sb[:]))
        cand_codes = keep.tile([P, C], I32, align_bytes=64)
        nc.vector.tensor_copy(cand_codes[:].bitcast(U32), x_codes[:].bitcast(U32).indirect(cand_sb[:]))
        cand_scales = keep.tile([P, C], U8, align_bytes=64)
        nc.vector.tensor_copy(
            cand_scales[:].rearrange("p (t m) -> p t m", t=PACK), cand_bytes[:].rearrange("p (m t) -> p t m", t=PACK)
        )
        cand_codes_dealt = keep.tile([P, C], I32, align_bytes=64)
        nc.vector.tensor_copy(
            cand_codes_dealt[:].rearrange("p (t a i) -> p a t i", t=PACK, i=4),
            cand_codes[:].rearrange("p (a i t) -> p a t i", t=PACK, i=4),
        )
        place_scale_rows(cand_scales)

        z_codes = keep.tile([P, S], I32, align_bytes=64)
        z_scales = keep.tile([P, S], U8, align_bytes=64)
        s = [keep.tile([P, S], F32, name=f"s{t}") for t in range(PACK)]
        z_early = keep.tile([P, EARLY * PACK], BF16, align_bytes=64)
        z_last = keep.tile([P, QUARTER * PACK], BF16, tag="z_last", align_bytes=64)

        batches = [(0, HALF, t, 1) for t in range(PACK)]
        batches = batches + [(first, QUARTER, t, 2) for first in (HALF, EARLY) for t in (0, 2)]
        batch_values = HALF
        ea, upper, lower, most, least, spread = {}, {}, {}, {}, {}, {}

        def ends_columns(step):
            first, width, t0, tiles = batches[step]
            return t0 + tiles == PACK

        def fetch_exp(step):
            first, width, t0, tiles = batches[step]
            ea[step] = keep.tile([P, tiles, width * MEMBERS], F32, name=f"ea{step}")
            for t in range(t0, t0 + tiles):
                nc.scalar.activation(
                    ea[step][:, t - t0, :],
                    y[t][:].indirect(entries(n1_sb, first * MEMBERS, width * MEMBERS)),
                    ACT.Exp,
                    bias=bias[:, t : t + 1],
                    scale=tau_sb[:, t : t + 1],
                )

        def pair_up(step, results, op, name):
            members = ea[step][:].rearrange("p t (a i m) -> p (t a) i m", i=PAIR, m=MEMBERS)
            results[step] = ring.tile([P, batch_values // PAIR, 2, PAIR], F32, name=name)
            nc.vector.tensor_tensor(
                results[step][:].rearrange("p a h i -> p a i h"), members[:, :, :, 0:2], members[:, :, :, 2:4], op
            )

        def finish_pairs(step, pairs, results, op, name):
            results[step] = ring.tile([P, batch_values], F32, name=name)
            nc.vector.tensor_tensor(
                results[step][:].rearrange("p (a i) -> p a i", i=PAIR),
                pairs[step][:, :, 0, :],
                pairs[step][:, :, 1, :],
                op,
            )

        def subtract(step):
            first, width, t0, tiles = batches[step]
            if t0 == 0:
                spread[first] = keep.tile([P, PACK * width], F32, name=f"spread{first}")
            nc.vector.tensor_tensor(
                spread[first][:, t0 * width : (t0 + tiles) * width], most[step][:], least[step][:], ALU.subtract
            )

        def make_z(step):
            first, width, t0, tiles = batches[step]
            target = z_last[:] if first == EARLY else z_early[:, first * PACK : (first + width) * PACK]
            nc.vector.tensor_tensor(
                target.rearrange("p (a i t) -> p a t i", i=PAIR, t=PACK),
                spread[first][:].rearrange("p (t a i) -> p a t i", t=PACK, i=PAIR),
                y_weighted[:, :, first : first + width].rearrange("p t (a i) -> p a t i", i=PAIR),
                ALU.mult,
            )

        def score(z_tile, first, widths, bank_tag):
            cols = slice(first, first + sum(widths))
            nc.vector.quantize_mx(out=z_codes[:, cols].bitcast(FP8X4), scales=z_scales[:, cols], in_=z_tile[:])
            for t in range(PACK):
                bank = psum.tile([P, sum(widths)], F32, name=f"scores{first}_{t}", tag=f"{bank_tag}{t}")
                start = 0
                for width in widths:
                    moving = slice(first + start, first + start + width)
                    nc.tensor.matmul_mx(
                        out=bank[:, start : start + width],
                        lhsT=cand_codes_dealt[:, P * t : P * (t + 1)].bitcast(FP8X4),
                        lhsT_scale=cand_scales[:, P * t : P * (t + 1)],
                        rhs=z_codes[:, moving].bitcast(FP8X4),
                        rhs_scale=z_scales[:, moving],
                        start=True,
                        stop=True,
                    )
                    start = start + width
                nc.scalar.activation(s[t][:, cols], bank[:], ACT.Copy, scale=0.0625)

        n_steps = len(batches)
        for step in range(n_steps + 1):
            if step < n_steps:
                fetch_exp(step)
                pair_up(step, upper, ALU.max, "upper")
            if step > 0:
                subtract(step - 1)
            if step < n_steps:
                pair_up(step, lower, ALU.min, "lower")
            if step > 0 and ends_columns(step - 1):
                make_z(step - 1)
            if step < n_steps:
                finish_pairs(step, upper, most, ALU.max, "most")
            if step > 0 and ends_columns(step - 1) and batches[step - 1][0] == HALF:
                score(z_early, 0, (HALF, QUARTER), "s_bank")
            if step < n_steps:
                finish_pairs(step, lower, least, ALU.min, "least")
        score(z_last, EARLY, (QUARTER,), "y_bank")

        for t in range(2, PACK):
            fetch_tab_on_scalar(factor[:, t, :], t, n2_sb)
        term_3 = keep.tile([P, S], F32, tag="z_last", align_bytes=64)
        nc.vector.tensor_copy(term_3[:], tab_sb[3][:].indirect(n3_sb[:]))
        term_2 = keep.tile([P, S], F32)
        fetch_tab_on_scalar(term_2[:], 2, n3_sb)

        out_rows = out_0.rearrange("(p t) j -> p t j", t=PACK)
        out_words = out_1[0].rearrange("p c r -> p (c r)").bitcast(I32)
        out_scales = keep.tile([P, S], U8, align_bytes=64)

        def pick_on_scalar(dst, t, h):
            nc.scalar.activation(dst, s[t][:].indirect(entries(n4_sb, h * HALF, HALF)), ACT.Copy)

        def add_terms(h, product):
            cols = slice(h * HALF, (h + 1) * HALF)
            result = keep.tile([P, PACK, HALF], F32, name=f"result{h}")
            nc.vector.tensor_tensor(result[:, 0:2, :], product[:, 0:2, :], term_low[:, :, cols], ALU.add)
            nc.sync.dma_start(out_rows[:, 0:2, cols], result[:, 0:2, :])
            nc.vector.tensor_tensor(result[:, 3, :], product[:, 3, :], term_3[:, cols], ALU.add)
            nc.vector.tensor_tensor(result[:, 2, :], product[:, 2, :], term_2[:, cols], ALU.add)
            nc.sync.dma_start(out_rows[:, 2:4, cols], result[:, 2:4, :])
            return result

        def hand_out(h, result, shares):
            cols = slice(h * HALF, (h + 1) * HALF)
            rounded = keep.tile([P, HALF * PACK], BF16, name=f"rounded{h}", align_bytes=64)
            for copy, first, end in shares:
                copy(
                    rounded[:, first * PACK : end * PACK].rearrange("p (a i t) -> p a t i", i=PAIR, t=PACK),
                    result[:, :, first:end].rearrange("p t (a i) -> p a t i", i=PAIR),
                )
            codes = keep.tile([P, HALF], I32, name=f"out_codes{h}", align_bytes=64)
            nc.vector.quantize_mx(out=codes[:].bitcast(FP8X4), scales=out_scales[:, cols], in_=rounded[:])
            nc.sync.dma_start(out_words[:, cols], codes[:])

        product0 = keep.tile([P, PACK, HALF], F32)
        picked0 = keep.tile([P, 2, HALF], F32)
        picked1 = keep.tile([P, PACK, HALF], F32)
        product1 = keep.tile([P, PACK, HALF], F32)
        for t in range(2):
            nc.vector.tensor_tensor(
                product0[:, t, :], s[t][:].indirect(entries(n4_sb, 0, HALF)), factor[:, t, :HALF], ALU.mult
            )
        for t in range(2, PACK):
            pick_on_scalar(picked0[:, t - 2, :], t, 0)
        nc.vector.tensor_tensor(product0[:, 2:4, :], picked0[:], factor[:, 2:4, :HALF], ALU.mult)
        for t in range(PACK):
            pick_on_scalar(picked1[:, t, :], t, 1)
        result0 = add_terms(0, product0)
        for both in (slice(0, 2), slice(2, 4)):
            nc.vector.tensor_tensor(product1[:, both, :], picked1[:, both, :], factor[:, both, HALF:], ALU.mult)
        result1 = add_terms(1, product1)
        hand_out(0, result0, [(nc.scalar.copy, 0, HALF)])
        hand_out(1, result1, [(nc.vector.tensor_copy, 0, ROUNDED_ON_VECTOR), (nc.scalar.copy, ROUNDED_ON_VECTOR, HALF)])

        for q in range(P // QUADRANT):
            queue = nc.sync if q % 2 == 0 else nc.scalar
            queue.dma_start(
                out_2[0, PACK * q : PACK * (q + 1), :].bitcast(I32),
                out_scales[QUADRANT * q : QUADRANT * q + PACK, :].bitcast(I32),
            )
